import numpy as np
import ml_dtypes

BF16 = ml_dtypes.bfloat16


def bf(x):
    return np.asarray(x, np.float32).astype(BF16)


def f32(x):
    return np.asarray(x, np.float32)


def f64(x):
    return np.asarray(x).astype(np.float64)


def striped(idx):
    return np.concatenate([l.reshape(-1, 16).T for l in idx])


def rows(idx, k):
    return np.tile(np.repeat(idx, 16, axis=0), (k // (16 * 8), 1))


def look(tab, idx):
    return np.take_along_axis(f64(tab), rows(idx, len(tab)), axis=1)


K, S, D, V, N, M = 256, 2048, 4, 512, 2048, 256


def setup_inputs():
    return {"tab": f32(np.random.standard_normal((K, S))), "x0": f32(np.random.standard_normal((K, V))), "w": bf(np.random.standard_normal((K, M)) / np.sqrt(K)), "offs": striped(np.stack([np.random.permutation(S)[:N] for _ in range(8)]))}


def reference(tab, x0, w, offs):
    idx = np.stack([g.T.reshape(-1) for g in np.split(offs, 8)])
    x = f64(x0)
    for d in range(D):
        x = np.maximum(x, look(tab, idx[:, d * V:(d + 1) * V]))
    y = f64(w).T @ x
    return y

@@ -1,0 +1,59 @@
+import concourse.mybir as mybir
+
+F32, BF16, U16 = mybir.dt.float32, mybir.dt.bfloat16, mybir.dt.uint16
+MAX = mybir.AluOpType.max
+
+P = 128
+R = 256
+S = 2048
+D = 4
+V = 512
+M = 256
+LIST_COLUMNS = V // 16
+
+FLOPS = 2 * R * M * V
+
+
+def tile_lookup_pool_max_none_kernel(tc, tab, x0, w, offs, out):
+    nc = tc.nc
+    blocks, outputs = R // P, M // P
+    with (
+        tc.tile_pool(name="held", bufs=1) as held,
+        tc.tile_pool(name="running", bufs=2) as running_pool,
+        tc.psum_pool(name="psum", bufs=1) as psum,
+    ):
+        offsets = held.tile([P, D * LIST_COLUMNS], U16, name="offsets")
+        nc.sync.dma_start(offsets[:], offs)
+        windows, centres = [], []
+        for b in range(blocks):
+            window = held.tile([P, S], F32, name=f"window{b}")
+            nc.sync.dma_start(window[:], tab[b * P : (b + 1) * P, :])
+            windows.append(window)
+            centre = held.tile([P, V], F32, name=f"centre{b}")
+            queue = nc.scalar if b == 0 else nc.sync
+            queue.dma_start(centre[:], x0[b * P : (b + 1) * P, :])
+            centres.append(centre)
+        weights = held.tile([P, blocks, M], BF16, name="weights")
+        nc.sync.dma_start(weights[:], w.rearrange("(b p) m -> p b m", p=P))
+
+        sums = [psum.tile([P, V], F32, name=f"sums{m}") for m in range(outputs)]
+        for b in range(blocks):
+            running = centres[b]
+            for d in range(D):
+                larger = running_pool.tile([P, V], F32, name="larger")
+                entries = offsets[:, d * LIST_COLUMNS : (d + 1) * LIST_COLUMNS]
+                nc.vector.tensor_tensor(larger[:], windows[b][:].indirect(entries), running[:], MAX)
+                running = larger
+            x = held.tile([P, V], BF16, name=f"x{b}")
+            nc.scalar.copy(x[:], running[:])
+            for m in range(outputs):
+                nc.tensor.matmul(
+                    sums[m][:], weights[:, b, m * P : (m + 1) * P], x[:], start=(b == 0), stop=(b == blocks - 1)
+                )
+        for m in range(outputs):
+            result = held.tile([P, V], F32, name=f"result{m}")
+            if m % 2 == 0:
+                nc.scalar.copy(result[:], sums[m][:])
+            else:
+                nc.vector.tensor_copy(result[:], sums[m][:])
+            nc.sync.dma_start(out[m * P : (m + 1) * P, :], result[:])

@@ -9,6 +9,8 @@ S = 2048
 D = 4
 V = 512
 M = 256
+CHAINS = 2
+HALF = V // 2
 LIST_COLUMNS = V // 16
 
 FLOPS = 2 * R * M * V
@@ -17,43 +19,49 @@ FLOPS = 2 * R * M * V
 def tile_lookup_pool_max_none_kernel(tc, tab, x0, w, offs, out):
     nc = tc.nc
     blocks, outputs = R // P, M // P
+    halves = [slice(0, HALF), slice(HALF, V)]
     with (
         tc.tile_pool(name="held", bufs=1) as held,
-        tc.tile_pool(name="running", bufs=2) as running_pool,
         tc.psum_pool(name="psum", bufs=1) as psum,
     ):
         offsets = held.tile([P, D * LIST_COLUMNS], U16, name="offsets")
         nc.sync.dma_start(offsets[:], offs)
         windows, centres = [], []
         for b in range(blocks):
-            window = held.tile([P, S], F32, name=f"window{b}")
-            nc.sync.dma_start(window[:], tab[b * P : (b + 1) * P, :])
-            windows.append(window)
             centre = held.tile([P, V], F32, name=f"centre{b}")
             queue = nc.scalar if b == 0 else nc.sync
             queue.dma_start(centre[:], x0[b * P : (b + 1) * P, :])
             centres.append(centre)
+            window = held.tile([P, S], F32, name=f"window{b}")
+            nc.sync.dma_start(window[:], tab[b * P : (b + 1) * P, :])
+            windows.append(window)
         weights = held.tile([P, blocks, M], BF16, name="weights")
         nc.sync.dma_start(weights[:], w.rearrange("(b p) m -> p b m", p=P))
 
-        sums = [psum.tile([P, V], F32, name=f"sums{m}") for m in range(outputs)]
+        sums = [[psum.tile([P, HALF], F32, name=f"sums{h}_{m}") for m in range(outputs)] for h in range(len(halves))]
         for b in range(blocks):
-            running = centres[b]
+            partial = [centres[b]] * CHAINS
             for d in range(D):
-                larger = running_pool.tile([P, V], F32, name="larger")
+                larger = held.tile([P, V], F32, name=f"larger{b}_{d}")
                 entries = offsets[:, d * LIST_COLUMNS : (d + 1) * LIST_COLUMNS]
-                nc.vector.tensor_tensor(larger[:], windows[b][:].indirect(entries), running[:], MAX)
-                running = larger
+                nc.vector.tensor_tensor(larger[:], windows[b][:].indirect(entries), partial[d % CHAINS][:], MAX)
+                partial[d % CHAINS] = larger
             x = held.tile([P, V], BF16, name=f"x{b}")
-            nc.scalar.copy(x[:], running[:])
+            for h, columns in enumerate(halves):
+                nc.vector.tensor_tensor(x[:, columns], partial[0][:, columns], partial[1][:, columns], MAX)
+                for m in range(outputs):
+                    nc.tensor.matmul(
+                        sums[h][m][:],
+                        weights[:, b, m * P : (m + 1) * P],
+                        x[:, columns],
+                        start=(b == 0),
+                        stop=(b == blocks - 1),
+                    )
+        for h, columns in enumerate(halves):
             for m in range(outputs):
-                nc.tensor.matmul(
-                    sums[m][:], weights[:, b, m * P : (m + 1) * P], x[:], start=(b == 0), stop=(b == blocks - 1)
-                )
-        for m in range(outputs):
-            result = held.tile([P, V], F32, name=f"result{m}")
-            if m % 2 == 0:
-                nc.scalar.copy(result[:], sums[m][:])
-            else:
-                nc.vector.tensor_copy(result[:], sums[m][:])
-            nc.sync.dma_start(out[m * P : (m + 1) * P, :], result[:])
+                result = held.tile([P, HALF], F32, name=f"result{h}_{m}")
+                if m % 2 == 0:
+                    nc.scalar.copy(result[:], sums[h][m][:])
+                else:
+                    nc.vector.tensor_copy(result[:], sums[h][m][:])
+                nc.sync.dma_start(out[m * P : (m + 1) * P, columns], result[:])

@@ -11,6 +11,7 @@ V = 512
 M = 256
 CHAINS = 2
 HALF = V // 2
+WARM_UPS = 3 * D
 LIST_COLUMNS = V // 16
 
 FLOPS = 2 * R * M * V
@@ -39,6 +40,8 @@ def tile_lookup_pool_max_none_kernel(tc, tab, x0, w, offs, out):
         nc.sync.dma_start(weights[:], w.rearrange("(b p) m -> p b m", p=P))
 
         sums = [[psum.tile([P, HALF], F32, name=f"sums{h}_{m}") for m in range(outputs)] for h in range(len(halves))]
+        unread = psum.tile([P, V], F32, name="unread")
+
         for b in range(blocks):
             partial = [centres[b]] * CHAINS
             for d in range(D):
@@ -57,6 +60,9 @@ def tile_lookup_pool_max_none_kernel(tc, tab, x0, w, offs, out):
                         start=(b == 0),
                         stop=(b == blocks - 1),
                     )
+            if b < blocks - 1:
+                for warm_up in range(WARM_UPS):
+                    nc.tensor.matmul(unread[:], weights[:, b, :P], x[:], start=True, stop=True)
         for h, columns in enumerate(halves):
             for m in range(outputs):
                 result = held.tile([P, HALF], F32, name=f"result{h}_{m}")

import concourse.mybir as mybir

F32, BF16, U16 = mybir.dt.float32, mybir.dt.bfloat16, mybir.dt.uint16
MAX = mybir.AluOpType.max

P = 128
R = 256
S = 2048
D = 4
V = 512
M = 256
CHAINS = 2
HALF = V // 2
WARM_UPS = 3 * D
LIST_COLUMNS = V // 16

FLOPS = 2 * R * M * V


def tile_lookup_pool_max_none_kernel(tc, tab, x0, w, offs, out):
    nc = tc.nc
    blocks, outputs = R // P, M // P
    halves = [slice(0, HALF), slice(HALF, V)]
    with (
        tc.tile_pool(name="held", bufs=1) as held,
        tc.psum_pool(name="psum", bufs=1) as psum,
    ):
        offsets = held.tile([P, D * LIST_COLUMNS], U16, name="offsets")
        nc.sync.dma_start(offsets[:], offs)
        windows, centres = [], []
        for b in range(blocks):
            centre = held.tile([P, V], F32, name=f"centre{b}")
            queue = nc.scalar if b == 0 else nc.sync
            queue.dma_start(centre[:], x0[b * P : (b + 1) * P, :])
            centres.append(centre)
            window = held.tile([P, S], F32, name=f"window{b}")
            nc.sync.dma_start(window[:], tab[b * P : (b + 1) * P, :])
            windows.append(window)
        weights = held.tile([P, blocks, M], BF16, name="weights")
        nc.sync.dma_start(weights[:], w.rearrange("(b p) m -> p b m", p=P))

        sums = [[psum.tile([P, HALF], F32, name=f"sums{h}_{m}") for m in range(outputs)] for h in range(len(halves))]
        unread = psum.tile([P, V], F32, name="unread")

        for b in range(blocks):
            partial = [centres[b]] * CHAINS
            for d in range(D):
                larger = held.tile([P, V], F32, name=f"larger{b}_{d}")
                entries = offsets[:, d * LIST_COLUMNS : (d + 1) * LIST_COLUMNS]
                nc.vector.tensor_tensor(larger[:], windows[b][:].indirect(entries), partial[d % CHAINS][:], MAX)
                partial[d % CHAINS] = larger
            x = held.tile([P, V], BF16, name=f"x{b}")
            for h, columns in enumerate(halves):
                nc.vector.tensor_tensor(x[:, columns], partial[0][:, columns], partial[1][:, columns], MAX)
                for m in range(outputs):
                    nc.tensor.matmul(
                        sums[h][m][:],
                        weights[:, b, m * P : (m + 1) * P],
                        x[:, columns],
                        start=(b == 0),
                        stop=(b == blocks - 1),
                    )
            if b < blocks - 1:
                for warm_up in range(WARM_UPS):
                    nc.tensor.matmul(unread[:], weights[:, b, :P], x[:], start=True, stop=True)
        for h, columns in enumerate(halves):
            for m in range(outputs):
                result = held.tile([P, HALF], F32, name=f"result{h}_{m}")
                if m % 2 == 0:
                    nc.scalar.copy(result[:], sums[h][m][:])
                else:
                    nc.vector.tensor_copy(result[:], sums[h][m][:])
                nc.sync.dma_start(out[m * P : (m + 1) * P, columns], result[:])
